import numpy as np
import ml_dtypes


def mxq(x, axis, fmt="e4m3"):
    dtype, down = {"e4m3": (ml_dtypes.float8_e4m3fn, 7), "e5m2": (ml_dtypes.float8_e5m2, 14)}[fmt]
    v = np.moveaxis(np.asarray(x, np.float32).astype(ml_dtypes.bfloat16).astype(np.float64), axis, -1)
    blocks = v.reshape(v.shape[:-1] + (-1, 32))
    amax = np.abs(blocks).max(-1, keepdims=True)
    byte = np.maximum(np.where(amax > 0, np.frexp(amax)[1] - 1 + 127, 0) - down, 1)
    scale = np.exp2(byte - 127.0)
    codes = (blocks / scale).astype(np.float32).astype(dtype).astype(np.float64)
    return np.moveaxis((codes * scale).reshape(v.shape), -1, axis)


WIDE = False


def mx_kscale(k):
    if not WIDE:
        return np.ones(k)
    levels = np.array([10, -10, 5, -5, 0])
    if k % 512:
        return np.exp2(np.random.permutation(np.resize(levels, k // 32))).repeat(32)
    a = np.empty((k // 512, 16))
    for p in range(k // 512):
        a[p, :8] = np.random.permutation(np.resize(levels, 8))
        for g in range(8):
            far = levels[np.abs(levels - a[p, g]) >= 10]
            a[p, g + 8] = far[np.random.randint(len(far))]
    return np.exp2(a.ravel()).repeat(32)


def f64(x):
    return np.asarray(x).astype(np.float64)


def striped(idx):
    return np.tile(idx.reshape(-1, 16).T, (8, 1)).astype(np.uint16)


def unstriped(offs):
    return offs[:16].T.reshape(-1).astype(np.int64)


def pack_weight(w):
    k, n = w.shape
    w = f64(np.asarray(w, np.float32).astype(ml_dtypes.bfloat16)).reshape(k // 32, 32, n)
    amax = np.abs(w).max(1)
    byte = np.clip(np.where(amax > 0, np.frexp(amax)[1] - 1 + 127 - 7, 1), 1, 254)
    scaled = (w * np.exp2(127.0 - byte)[:, None, :]).reshape(k, n).astype(np.float32)
    words = np.ascontiguousarray(scaled.reshape(k // 512, 128, 4, n).transpose(0, 1, 3, 2)).astype(ml_dtypes.float8_e4m3fn).view(np.uint8)
    return words, np.ascontiguousarray(byte.astype(np.uint8).reshape(k // 512, 16, n))


def unpack_weight(words, scales):
    g, p, n, _ = words.shape
    vals = np.ascontiguousarray(words).view(ml_dtypes.float8_e4m3fn).astype(np.float64) * np.repeat(np.exp2(scales.astype(np.float64) - 127.0), 8, axis=1)[..., None]
    return vals.transpose(0, 1, 3, 2).reshape(g * 512, n)


E2M1 = np.array([0.0, 0.5, 1.0, 1.5, 2.0, 3.0, 4.0, 6.0, -0.0, -0.5, -1.0, -1.5, -2.0, -3.0, -4.0, -6.0])


def pack_fp4(w):
    k, n = w.shape
    w = f64(np.asarray(w, np.float32).astype(ml_dtypes.bfloat16)).reshape(k // 32, 32, n)
    amax = np.abs(w).max(1)
    mant, ex = np.frexp(amax / 6.0)
    byte = np.clip(np.where(amax > 0, np.where(mant > 0.5, ex, ex - 1) + 127, 1), 1, 254)
    scaled = (w * np.exp2(127.0 - byte)[:, None, :]).reshape(k, n).astype(np.float32)
    c = np.ascontiguousarray(scaled.reshape(k // 512, 128, 4, n).transpose(0, 1, 3, 2)).astype(ml_dtypes.float4_e2m1fn).view(np.uint8) & 0xF
    words = (c[..., 0::2] | (c[..., 1::2] << 4)).reshape(k // 512, 128, 2 * n)
    return np.ascontiguousarray(words), np.ascontiguousarray(byte.astype(np.uint8).reshape(k // 512, 16, n))


def unpack_fp4(words, scales):
    g, _, n = scales.shape
    words = np.ascontiguousarray(words).reshape(g, 128, n, 2)
    nib = np.empty((g, 128, n, 4), np.uint8)
    nib[..., 0::2] = words & 0xF
    nib[..., 1::2] = words >> 4
    vals = E2M1[nib] * np.repeat(np.exp2(scales.astype(np.float64) - 127.0), 8, axis=1)[..., None]
    return vals.transpose(0, 1, 3, 2).reshape(g * 512, n)


def relu(v):
    return np.maximum(v, 0.0)


K, T, S, N, H = 1024, 1024, 512, 256, 512


def setup_inputs():
    n = np.random.standard_normal
    s = mx_kscale(K)[:, None]
    u = mx_kscale(H)
    packed_xT = pack_weight(n((K, T)) * s)
    packed_w1 = pack_fp4(n((K, H)) / np.sqrt(K) / s)
    packed_w2 = pack_fp4(n((K, H)) / np.sqrt(K) / s)
    packed_w3 = pack_fp4(n((H, N)) / np.sqrt(H) / u[:, None])
    return {
        "x_words": packed_xT[0],
        "x_scales": packed_xT[1],
        "w1_words": packed_w1[0],
        "w1_scales": packed_w1[1],
        "w2_words": packed_w2[0],
        "w2_scales": packed_w2[1],
        "pen": (np.random.uniform(1.0, 2.0, (H, 1))).astype(np.float32),
        "unit": (np.random.uniform(0.6, 1.4, (H, 1)) * u[:, None]).astype(np.float32),
        "w3_words": packed_w3[0],
        "w3_scales": packed_w3[1],
        "offs": striped(np.random.permutation(T)[:S]),
        "nb1": striped(np.random.permutation(S)),
        "nb2": striped(np.random.permutation(S)),
    }


def reference(x_words, x_scales, w1_words, w1_scales, w2_words, w2_scales, pen, unit, w3_words, w3_scales, offs, nb1, nb2):
    xq = unpack_weight(x_words, x_scales)[:, unstriped(offs)]
    dm = unpack_fp4(w1_words, w1_scales).T @ xq
    dem = np.log(np.exp(dm) + 1.0)
    st = unpack_fp4(w2_words, w2_scales).T @ xq
    stk = np.log(np.exp(st) + 1.0)
    shrt = relu(dem - stk)
    exc = relu(stk - dem)
    e1 = exc[:, unstriped(nb1)]
    tr1 = np.minimum(shrt, e1)
    shrt2 = shrt - tr1
    e2 = exc[:, unstriped(nb2)]
    tr2 = np.minimum(shrt2, 0.5 * e2)
    lost = shrt2 - tr2
    cost = f64(pen) * lost + 0.3 * exc + 0.5 * (tr1 + tr2)
    hid = f64(unit) * (tr1 + tr2 - (0.3 * cost[:, unstriped(nb1)]))
    return unpack_fp4(w3_words, w3_scales).T @ mxq(hid, 0, "e4m3")

@@ -1,0 +1,277 @@
+from contextlib import ExitStack
+
+import concourse.mybir as mybir
+from concourse.masks import make_identity
+
+F32 = mybir.dt.float32
+BF16 = mybir.dt.bfloat16
+I32 = mybir.dt.int32
+U32 = mybir.dt.uint32
+U16 = mybir.dt.uint16
+U8 = mybir.dt.uint8
+FP8X4 = mybir.dt.float8_e4m3fn_x4
+FP4X4 = mybir.dt.float4_e2m1fn_x4
+ALU = mybir.AluOpType
+ACT = mybir.ActivationFunctionType
+
+K, T, S, N, H = 1024, 1024, 512, 256, 512
+P = 128
+PACK = 4
+PASSES = K // (P * PACK)
+BLOCKS = S // P
+SPARE = 16
+FLOOR = 2.0 ** -60
+KNEE = 20.0
+HALF = S // 2
+FLOPS = 2 * (2 * K * H * S + H * N * S)
+
+
+def tile_picked_ynewsv_mov_p_kernel(tc, x_words, x_scales, w1_words, w1_scales, w2_words, w2_scales, pen, unit,
+                        w3_words, w3_scales, offs, nb1, nb2, out):
+    nc = tc.nc
+    with ExitStack() as ctx:
+        lists = ctx.enter_context(tc.tile_pool(name="lists", bufs=1))
+        keep = ctx.enter_context(tc.tile_pool(name="keep", bufs=1))
+        psum = ctx.enter_context(tc.psum_pool(name="psum", bufs=1))
+
+        offs_t = lists.tile([P, S // 16], U16, name="offs_t")
+        nb1_t = lists.tile([P, S // 16], U16, name="nb1_t")
+        nb2_t = lists.tile([P, S // 16], U16, name="nb2_t")
+
+        xw = keep.tile([P, PASSES, T], I32, name="xw", align_bytes=64)
+        xs = keep.tile([P, PASSES, T], U8, name="xs", align_bytes=64)
+        ww = [keep.tile([P, PASSES, 2 * H], U8, name=f"ww{m}", align_bytes=64) for m in range(2)]
+        ws = [keep.tile([P, PASSES, H], U8, name=f"ws{m}", align_bytes=64) for m in range(2)]
+        w3w = keep.tile([P, 2 * N], U8, name="w3w", align_bytes=64)
+        w3s = keep.tile([P, N], U8, name="w3s", align_bytes=64)
+        pen_t = keep.tile([P, PACK], F32, name="pen_t")
+        unit_t = keep.tile([P, PACK], F32, name="unit_t")
+
+        def load_scales(queue, plane, src, quads):
+            for q in quads:
+                queue.dma_start(out=plane[32 * q:32 * q + 4].bitcast(I32),
+                                in_=src[:, 4 * q:4 * q + 4, :].rearrange("o r c -> r o c").bitcast(I32))
+
+        def load_words():
+            nc.sync.dma_start(out=xw[:], in_=x_words.rearrange("o p c t -> p o (c t)").bitcast(I32))
+
+        def load_w(queue, m, src):
+            queue.dma_start(out=ww[m][:].bitcast(I32), in_=src.rearrange("o p c -> p o c").bitcast(I32))
+
+        nc.gpsimd.memset(xs[:].bitcast(I32), 0)
+        nc.gpsimd.memset(ws[0][:].bitcast(I32), 0)
+        nc.vector.memset(ws[1][:].bitcast(I32), 0)
+        nc.vector.memset(w3s[:].bitcast(I32), 0)
+        load_scales(nc.gpsimd, ws[0], w1_scales, [0, 1, 2])
+        nc.sync.dma_start(offs_t[:], offs)
+        nc.sync.dma_start(nb2_t[:], nb2)
+        load_scales(nc.sync, xs, x_scales, range(4))
+        load_words()
+        load_w(nc.sync, 1, w2_words)
+        load_scales(nc.sync, ws[1], w2_scales, range(4))
+        load_w(nc.sync, 0, w1_words)
+        load_scales(nc.sync, ws[0], w1_scales, [3])
+        nc.sync.dma_start(nb1_t[:], nb1)
+        nc.sync.dma_start(out=pen_t[:], in_=pen.rearrange("(p t) one -> p (t one)", t=PACK))
+        nc.sync.dma_start(out=unit_t[:], in_=unit.rearrange("(p t) one -> p (t one)", t=PACK))
+        nc.sync.dma_start(out=w3w[:].bitcast(I32), in_=w3_words[0].bitcast(I32))
+        for q in range(4):
+            nc.sync.dma_start(out=w3s[32 * q:32 * q + 4, :].bitcast(I32), in_=w3_scales[0, 4 * q:4 * q + 4, :].bitcast(I32))
+
+        ident = keep.tile([P, P], F32, name="ident")
+        make_identity(nc, ident[:])
+
+        exc = [keep.tile([P, S + SPARE], F32, name=f"exc{t}") for t in range(PACK)]
+        cost = [keep.tile([P, S + SPARE], F32, name=f"cost{t}") for t in range(PACK)]
+        for t in range(PACK):
+            nc.vector.memset(exc[t][:, S:], 0.0)
+            nc.vector.memset(cost[t][:, S:], 0.0)
+
+        c_gap = keep.tile([P, PACK], F32, name="c_gap")
+        c_met = keep.tile([P, PACK], F32, name="c_met")
+        c_cost = keep.tile([P, PACK], F32, name="c_cost")
+        nc.gpsimd.tensor_scalar(c_gap[:], pen_t[:], 1.25, 0.0, ALU.mult, ALU.add)
+        nc.gpsimd.tensor_scalar(c_met[:], pen_t[:], -1.25, 0.625, ALU.mult, ALU.add)
+        nc.gpsimd.tensor_scalar(c_cost[:], unit_t[:], -0.24, 0.0, ALU.mult, ALU.add)
+
+        gw = [keep.tile([P, S], U32, name=f"gw{o}", align_bytes=64) for o in range(PASSES)]
+        gs = [keep.tile([P, S], U8, name=f"gs{o}", align_bytes=64) for o in range(PASSES)]
+        for o in range(PASSES):
+            nc.vector.tensor_copy(gs[o][:], xs[:, o, :].indirect(offs_t[:]))
+        for lo, hi in [(0, 128), (128, 256), (256, 384), (384, 512)]:
+            for o in range(PASSES):
+                nc.vector.tensor_copy(gw[o][:, lo:hi], xw[:, o, :].bitcast(U32).indirect(offs_t[:, lo // 16:hi // 16]))
+
+        acc = {}
+        for b in range(BLOCKS):
+            for m in range(2):
+                acc[m, b] = psum.tile([P, H], F32, name=f"acc{m}{b}", tag=f"bank{2 * b + m}")
+        def product(m, b, o):
+            cols = slice(b * P, (b + 1) * P)
+            nc.tensor.matmul_mx(out=acc[m, b][:], lhsT=gw[o][:, cols].bitcast(FP8X4), lhsT_scale=gs[o][:, cols],
+                                rhs=ww[m][:, o, :].bitcast(FP4X4), rhs_scale=ws[m][:, o, :],
+                                start=(o == 0), stop=(o == PASSES - 1))
+
+        for b in range(BLOCKS):
+            for m in (1, 0):
+                for o in range(PASSES):
+                    product(m, b, o)
+
+        def dealt(m, b):
+            return acc[m, b][:].rearrange("j (p t) -> j t p", t=PACK)
+
+        sig = keep.tile([P, 2, BLOCKS, PACK, P], F32, name="sig")
+        lns = [keep.tile([P, 2, BLOCKS * P], F32, name=f"lns{t}") for t in range(PACK)]
+        soft = [keep.tile([P, 2, BLOCKS * P], F32, name=f"soft{t}") for t in range(PACK)]
+        over_b = [keep.tile([P, PACK, P], F32, name=f"over_b{b}") for b in range(BLOCKS)]
+        over = [keep.tile([P, PACK, P], F32, name=f"over{b}") for b in range(BLOCKS)]
+        for b in range(BLOCKS):
+            for m in (1, 0):
+                nc.scalar.activation(sig[:, m, b], dealt(m, b), ACT.Sigmoid, scale=-1.0)
+        for b in range(BLOCKS):
+            nc.vector.tensor_scalar(over_b[b][:], dealt(1, b), KNEE, None, ALU.max)
+            nc.vector.scalar_tensor_tensor(over[b][:], dealt(0, b), KNEE, over_b[b][:], ALU.max, ALU.subtract)
+
+        gap = [psum.tile([P, S], F32, name=f"gap{t}", tag=f"bank{2 * t + 1}") for t in range(PACK)]
+        for b in range(BLOCKS):
+            for t in range(PACK):
+                nc.tensor.matmul(gap[t][:, b * P:(b + 1) * P], over[b][:, t, :], ident[:], start=(b == 0), stop=False, is_transpose=True)
+
+        def logs(t):
+            nc.scalar.activation(lns[t][:].rearrange("j m (b p) -> j m b p", p=P), sig[:, :, :, t, :], ACT.Ln, bias=FLOOR)
+            nc.vector.tensor_scalar(soft[t][:, 0], lns[t][:, 0], -1.0, KNEE, ALU.mult, ALU.min)
+            nc.vector.tensor_scalar(soft[t][:, 1], lns[t][:, 1], -KNEE, None, ALU.max)
+            for m in range(2):
+                for b in range(BLOCKS):
+                    nc.tensor.matmul(gap[t][:, b * P:(b + 1) * P], soft[t][:, m, b * P:(b + 1) * P], ident[:], start=False,
+                                     stop=(m == 1 and b == BLOCKS - 1), is_transpose=True)
+
+        first = [keep.tile([P, S], F32, name=f"first{t}") for t in range(PACK)]
+        half2 = [keep.tile([P, S], F32, name=f"half2_{t}") for t in range(PACK)]
+        offer = [keep.tile([P, S], F32, name=f"offer{t}") for t in range(PACK)]
+        base = [keep.tile([P, S], F32, name=f"base{t}") for t in range(PACK)]
+        low = [keep.tile([P, S], F32, name=f"low{t}") for t in range(PACK)]
+        met = [keep.tile([P, S], F32, name=f"met{t}") for t in range(PACK)]
+        far = [keep.tile([P, S], F32, name=f"far{t}") for t in range(PACK)]
+        hid = keep.tile([P, PACK, S], BF16, name="hid")
+
+        def exc_s(t):
+            nc.scalar.activation(exc[t][:, :S], gap[t][:], ACT.Relu, scale=-1.0)
+
+        def exc_v(t):
+            nc.vector.tensor_scalar(exc[t][:, :S], gap[t][:], -1.0, 0.0, ALU.mult, ALU.max)
+
+        def half_s(t):
+            nc.scalar.activation(half2[t][:], exc[t][:].indirect(nb2_t[:]), ACT.Copy, scale=0.5)
+
+        def first_s(t):
+            nc.scalar.activation(first[t][:], exc[t][:].indirect(nb1_t[:]), ACT.Copy)
+
+        def second_v(t):
+            nc.vector.tensor_copy(half2[t][:], exc[t][:].indirect(nb2_t[:]))
+
+        def offer_join(t):
+            nc.vector.scalar_tensor_tensor(offer[t][:], half2[t][:], 0.5, first[t][:], ALU.mult, ALU.add)
+
+        def offer_add(t):
+            nc.vector.tensor_tensor(offer[t][:], half2[t][:], first[t][:], ALU.add)
+
+        def offer_v(t):
+            nc.vector.tensor_tensor(offer[t][:], exc[t][:].indirect(nb1_t[:]), half2[t][:], ALU.add)
+
+        def based(t):
+            nc.vector.scalar_tensor_tensor(base[t][:], gap[t][:], c_gap[:, t:t + 1], exc[t][:, :S], ALU.mult, ALU.add)
+
+        def meet(t):
+            nc.vector.tensor_tensor(low[t][:], gap[t][:], offer[t][:], ALU.min)
+
+        def price(t):
+            nc.vector.scalar_tensor_tensor(cost[t][:, :S], low[t][:], c_met[:, t:t + 1], base[t][:], ALU.mult, ALU.add)
+
+        def metu(t):
+            nc.vector.tensor_scalar(met[t][:], low[t][:], 0.0, unit_t[:, t:t + 1], ALU.max, ALU.mult)
+
+        def fetch(t, lo=0, hi=S):
+            nc.scalar.activation(far[t][:, lo:hi], cost[t][:].indirect(nb1_t[:, lo // 16:hi // 16]), ACT.Copy)
+
+        def finish(t, lo=0, hi=S):
+            nc.vector.scalar_tensor_tensor(hid[:, t, lo:hi], far[t][:, lo:hi], c_cost[:, t:t + 1], met[t][:, lo:hi], ALU.mult, ALU.add)
+
+        chunks = [(0, 256), (256, 384), (384, 512)]
+        woven = [keep.tile([P, hi - lo, PACK], BF16, name=f"woven{lo}", align_bytes=64) for lo, hi in chunks]
+        codes = [keep.tile([P, hi - lo], U32, name=f"codes{lo}", align_bytes=64) for lo, hi in chunks]
+        scales = [keep.tile([P, hi - lo], U8, name=f"scales{lo}", align_bytes=64) for lo, hi in chunks]
+        res = [keep.tile([P, 2, hi - lo], F32, name=f"res{lo}") for lo, hi in chunks]
+
+        def weave(h):
+            lo, hi = chunks[h]
+            nc.vector.tensor_copy(woven[h][:], hid[:, :, lo:hi].rearrange("p t j -> p j t"))
+
+        def weave_s(h):
+            lo, hi = chunks[h]
+            nc.scalar.copy(woven[h][:], hid[:, :, lo:hi].rearrange("p t j -> p j t"))
+
+        def quant_v(h):
+            quant(h, nc.vector.tensor_copy)
+
+        def quant(h, move=nc.scalar.copy):
+            lo, hi = chunks[h]
+            nc.vector.quantize_mx(out=codes[h][:].bitcast(FP8X4), scales=scales[h][:], in_=woven[h][:].rearrange("p j t -> p (j t)"))
+            region = psum.tile([P, 2, hi - lo], F32, name=f"region{h}", tag=f"bank{2 * h}")
+            for r in range(2):
+                nc.tensor.matmul_mx(out=region[:, r, :], lhsT=w3w[:, r * 2 * P:(r + 1) * 2 * P].bitcast(FP4X4),
+                                    lhsT_scale=w3s[:, r * P:(r + 1) * P], rhs=codes[h][:].bitcast(FP8X4),
+                                    rhs_scale=scales[h][:], start=True, stop=True)
+            move(res[h][:], region[:])
+            nc.sync.dma_start(out=out[:, lo:hi].rearrange("(r p) j -> p r j", p=P), in_=res[h][:])
+
+        logs(0)
+        logs(1)
+        exc_v(0)
+        half_s(0)
+        based(0)
+        logs(2)
+        offer_v(0)
+        exc_s(1)
+        half_s(1)
+        based(1)
+        logs(3)
+        meet(0)
+        offer_v(1)
+        price(0)
+        exc_s(2)
+        half_s(2)
+        first_s(2)
+        meet(1)
+        metu(0)
+        fetch(0)
+        based(2)
+        price(1)
+        offer_add(2)
+        exc_s(3)
+        half_s(3)
+        first_s(3)
+        finish(0)
+        meet(2)
+        metu(1)
+        fetch(1)
+        based(3)
+        price(2)
+        offer_add(3)
+        finish(1)
+        meet(3)
+        metu(2)
+        fetch(2)
+        price(3)
+        finish(2)
+        metu(3)
+        fetch(3, 0, 256)
+        fetch(3, 256, 512)
+        finish(3, 0, 256)
+        weave(0)
+        finish(3, 256, 512)
+        quant(0)
+        weave(1)
+        weave(2)
+        quant(1)
+        quant_v(2)

@@ -59,10 +59,9 @@ def tile_picked_ynewsv_mov_p_kernel(tc, x_words, x_scales, w1_words, w1_scales, 
             queue.dma_start(out=ww[m][:].bitcast(I32), in_=src.rearrange("o p c -> p o c").bitcast(I32))
 
         nc.gpsimd.memset(xs[:].bitcast(I32), 0)
-        nc.gpsimd.memset(ws[0][:].bitcast(I32), 0)
         nc.vector.memset(ws[1][:].bitcast(I32), 0)
+        nc.vector.memset(ws[0][:].bitcast(I32), 0)
         nc.vector.memset(w3s[:].bitcast(I32), 0)
-        load_scales(nc.gpsimd, ws[0], w1_scales, [0, 1, 2])
         nc.sync.dma_start(offs_t[:], offs)
         nc.sync.dma_start(nb2_t[:], nb2)
         load_scales(nc.sync, xs, x_scales, range(4))
@@ -70,7 +69,7 @@ def tile_picked_ynewsv_mov_p_kernel(tc, x_words, x_scales, w1_words, w1_scales, 
         load_w(nc.sync, 1, w2_words)
         load_scales(nc.sync, ws[1], w2_scales, range(4))
         load_w(nc.sync, 0, w1_words)
-        load_scales(nc.sync, ws[0], w1_scales, [3])
+        load_scales(nc.sync, ws[0], w1_scales, range(4))
         nc.sync.dma_start(nb1_t[:], nb1)
         nc.sync.dma_start(out=pen_t[:], in_=pen.rearrange("(p t) one -> p (t one)", t=PACK))
         nc.sync.dma_start(out=unit_t[:], in_=unit.rearrange("(p t) one -> p (t one)", t=PACK))
@@ -112,8 +111,8 @@ def tile_picked_ynewsv_mov_p_kernel(tc, x_words, x_scales, w1_words, w1_scales, 
                                 rhs=ww[m][:, o, :].bitcast(FP4X4), rhs_scale=ws[m][:, o, :],
                                 start=(o == 0), stop=(o == PASSES - 1))
 
-        for b in range(BLOCKS):
-            for m in (1, 0):
+        for m in (1, 0):
+            for b in range(BLOCKS):
                 for o in range(PASSES):
                     product(m, b, o)
 
@@ -125,11 +124,12 @@ def tile_picked_ynewsv_mov_p_kernel(tc, x_words, x_scales, w1_words, w1_scales, 
         soft = [keep.tile([P, 2, BLOCKS * P], F32, name=f"soft{t}") for t in range(PACK)]
         over_b = [keep.tile([P, PACK, P], F32, name=f"over_b{b}") for b in range(BLOCKS)]
         over = [keep.tile([P, PACK, P], F32, name=f"over{b}") for b in range(BLOCKS)]
-        for b in range(BLOCKS):
-            for m in (1, 0):
+        for m in (1, 0):
+            for b in range(BLOCKS):
                 nc.scalar.activation(sig[:, m, b], dealt(m, b), ACT.Sigmoid, scale=-1.0)
         for b in range(BLOCKS):
             nc.vector.tensor_scalar(over_b[b][:], dealt(1, b), KNEE, None, ALU.max)
+        for b in range(BLOCKS):
             nc.vector.scalar_tensor_tensor(over[b][:], dealt(0, b), KNEE, over_b[b][:], ALU.max, ALU.subtract)
 
         gap = [psum.tile([P, S], F32, name=f"gap{t}", tag=f"bank{2 * t + 1}") for t in range(PACK)]
@@ -153,7 +153,9 @@ def tile_picked_ynewsv_mov_p_kernel(tc, x_words, x_scales, w1_words, w1_scales, 
         low = [keep.tile([P, S], F32, name=f"low{t}") for t in range(PACK)]
         met = [keep.tile([P, S], F32, name=f"met{t}") for t in range(PACK)]
         far = [keep.tile([P, S], F32, name=f"far{t}") for t in range(PACK)]
-        hid = keep.tile([P, PACK, S], BF16, name="hid")
+        chunks = [(0, 256), (256, 384), (384, 512)]
+        hid = [keep.tile([P, PACK, hi - lo], BF16, name=f"hid{lo}") for lo, hi in [(0, 256), (256, 512)]]
+        spans = [(0, 256), (256, 512)]
 
         def exc_s(t):
             nc.scalar.activation(exc[t][:, :S], gap[t][:], ACT.Relu, scale=-1.0)
@@ -195,21 +197,25 @@ def tile_picked_ynewsv_mov_p_kernel(tc, x_words, x_scales, w1_words, w1_scales, 
             nc.scalar.activation(far[t][:, lo:hi], cost[t][:].indirect(nb1_t[:, lo // 16:hi // 16]), ACT.Copy)
 
         def finish(t, lo=0, hi=S):
-            nc.vector.scalar_tensor_tensor(hid[:, t, lo:hi], far[t][:, lo:hi], c_cost[:, t:t + 1], met[t][:, lo:hi], ALU.mult, ALU.add)
+            nc.vector.scalar_tensor_tensor(hid[spans.index((lo, hi))][:, t, :], far[t][:, lo:hi], c_cost[:, t:t + 1], met[t][:, lo:hi], ALU.mult, ALU.add)
 
-        chunks = [(0, 256), (256, 384), (384, 512)]
         woven = [keep.tile([P, hi - lo, PACK], BF16, name=f"woven{lo}", align_bytes=64) for lo, hi in chunks]
         codes = [keep.tile([P, hi - lo], U32, name=f"codes{lo}", align_bytes=64) for lo, hi in chunks]
         scales = [keep.tile([P, hi - lo], U8, name=f"scales{lo}", align_bytes=64) for lo, hi in chunks]
         res = [keep.tile([P, 2, hi - lo], F32, name=f"res{lo}") for lo, hi in chunks]
 
+        def part(lo, hi):
+            for i, (a, b) in enumerate(spans):
+                if a <= lo and hi <= b:
+                    return hid[i][:, :, lo - a:hi - a]
+
         def weave(h):
             lo, hi = chunks[h]
-            nc.vector.tensor_copy(woven[h][:], hid[:, :, lo:hi].rearrange("p t j -> p j t"))
+            nc.vector.tensor_copy(woven[h][:], part(lo, hi).rearrange("p t j -> p j t"))
 
         def weave_s(h):
             lo, hi = chunks[h]
-            nc.scalar.copy(woven[h][:], hid[:, :, lo:hi].rearrange("p t j -> p j t"))
+            nc.scalar.copy(woven[h][:], part(lo, hi).rearrange("p t j -> p j t"))
 
         def quant_v(h):
             quant(h, nc.vector.tensor_copy)
@@ -227,51 +233,53 @@ def tile_picked_ynewsv_mov_p_kernel(tc, x_words, x_scales, w1_words, w1_scales, 
 
         logs(0)
         logs(1)
+        logs(2)
+        logs(3)
         exc_v(0)
         half_s(0)
         based(0)
-        logs(2)
-        offer_v(0)
         exc_s(1)
         half_s(1)
+        offer_v(0)
         based(1)
-        logs(3)
         meet(0)
-        offer_v(1)
-        price(0)
         exc_s(2)
         half_s(2)
-        first_s(2)
+        offer_v(1)
+        price(0)
         meet(1)
-        metu(0)
-        fetch(0)
         based(2)
-        price(1)
-        offer_add(2)
         exc_s(3)
         half_s(3)
         first_s(3)
-        finish(0)
-        meet(2)
-        metu(1)
-        fetch(1)
+        price(1)
+        offer_v(2)
         based(3)
-        price(2)
+        meet(2)
         offer_add(3)
-        finish(1)
+        price(2)
         meet(3)
-        metu(2)
-        fetch(2)
         price(3)
-        finish(2)
+        fetch(0)
+        fetch(1)
+        fetch(2)
+        fetch(3,0,256)
+        fetch(3,256,512)
+        metu(0)
+        metu(1)
+        metu(2)
         metu(3)
-        fetch(3, 0, 256)
-        fetch(3, 256, 512)
-        finish(3, 0, 256)
-        weave(0)
-        finish(3, 256, 512)
-        quant(0)
+        finish(0,0,256)
+        finish(1,0,256)
+        finish(2,0,256)
+        finish(3,0,256)
+        weave_s(0)
+        finish(0,256,512)
+        finish(1,256,512)
+        finish(2,256,512)
+        finish(3,256,512)
         weave(1)
+        quant(0)
         weave(2)
         quant(1)
         quant_v(2)

@@ -58,7 +58,7 @@ def tile_picked_ynewsv_mov_p_kernel(tc, x_words, x_scales, w1_words, w1_scales, 
         def load_w(queue, m, src):
             queue.dma_start(out=ww[m][:].bitcast(I32), in_=src.rearrange("o p c -> p o c").bitcast(I32))
 
-        nc.gpsimd.memset(xs[:].bitcast(I32), 0)
+        nc.vector.memset(xs[:].bitcast(I32), 0)
         nc.vector.memset(ws[1][:].bitcast(I32), 0)
         nc.vector.memset(ws[0][:].bitcast(I32), 0)
         nc.vector.memset(w3s[:].bitcast(I32), 0)
@@ -78,7 +78,8 @@ def tile_picked_ynewsv_mov_p_kernel(tc, x_words, x_scales, w1_words, w1_scales, 
             nc.sync.dma_start(out=w3s[32 * q:32 * q + 4, :].bitcast(I32), in_=w3_scales[0, 4 * q:4 * q + 4, :].bitcast(I32))
 
         ident = keep.tile([P, P], F32, name="ident")
-        make_identity(nc, ident[:])
+        nc.vector.memset(ident[:], 0.0)
+        make_identity(nc, ident[:], nomemset=True)
 
         exc = [keep.tile([P, S + SPARE], F32, name=f"exc{t}") for t in range(PACK)]
         cost = [keep.tile([P, S + SPARE], F32, name=f"cost{t}") for t in range(PACK)]
@@ -97,7 +98,7 @@ def tile_picked_ynewsv_mov_p_kernel(tc, x_words, x_scales, w1_words, w1_scales, 
         gs = [keep.tile([P, S], U8, name=f"gs{o}", align_bytes=64) for o in range(PASSES)]
         for o in range(PASSES):
             nc.vector.tensor_copy(gs[o][:], xs[:, o, :].indirect(offs_t[:]))
-        for lo, hi in [(0, 128), (128, 256), (256, 384), (384, 512)]:
+        for lo, hi in [(0, 128), (128, 256), (256, 512)]:
             for o in range(PASSES):
                 nc.vector.tensor_copy(gw[o][:, lo:hi], xw[:, o, :].bitcast(U32).indirect(offs_t[:, lo // 16:hi // 16]))
 
@@ -211,11 +212,11 @@ def tile_picked_ynewsv_mov_p_kernel(tc, x_words, x_scales, w1_words, w1_scales, 
 
         def weave(h):
             lo, hi = chunks[h]
-            nc.vector.tensor_copy(woven[h][:], part(lo, hi).rearrange("p t j -> p j t"))
+            nc.vector.tensor_copy(woven[h][:].rearrange("p (c i) t -> p c t i", i=4), part(lo, hi).rearrange("p t (c i) -> p c t i", i=4))
 
         def weave_s(h):
             lo, hi = chunks[h]
-            nc.scalar.copy(woven[h][:], part(lo, hi).rearrange("p t j -> p j t"))
+            nc.scalar.copy(woven[h][:].rearrange("p (c i) t -> p c t i", i=4), part(lo, hi).rearrange("p t (c i) -> p c t i", i=4))
 
         def quant_v(h):
             quant(h, nc.vector.tensor_copy)
@@ -237,14 +238,15 @@ def tile_picked_ynewsv_mov_p_kernel(tc, x_words, x_scales, w1_words, w1_scales, 
         logs(3)
         exc_v(0)
         half_s(0)
+        exc_v(1)
         based(0)
-        exc_s(1)
-        half_s(1)
         offer_v(0)
+        half_s(1)
         based(1)
         meet(0)
         exc_s(2)
         half_s(2)
+        first_s(2)
         offer_v(1)
         price(0)
         meet(1)
@@ -253,7 +255,7 @@ def tile_picked_ynewsv_mov_p_kernel(tc, x_words, x_scales, w1_words, w1_scales, 
         half_s(3)
         first_s(3)
         price(1)
-        offer_v(2)
+        offer_add(2)
         based(3)
         meet(2)
         offer_add(3)

@@ -1,3 +1,4 @@
+import math
 from contextlib import ExitStack
 
 import concourse.mybir as mybir
@@ -15,67 +16,71 @@ ALU = mybir.AluOpType
 ACT = mybir.ActivationFunctionType
 
 K, T, S, N, H = 1024, 1024, 512, 256, 512
+FLOPS = 2 * (2 * K * H * S + H * N * S)
+
 P = 128
 PACK = 4
 PASSES = K // (P * PACK)
 BLOCKS = S // P
+QUADRANTS = 4
+GROUP = 16
 SPARE = 16
-FLOOR = 2.0 ** -60
+DEMAND, STOCK = 0, 1
 KNEE = 20.0
-HALF = S // 2
-FLOPS = 2 * (2 * K * H * S + H * N * S)
+FLOOR = 2.0 ** -60
+RUN = 4
+
+WORD_SPANS = [(0, 128), (128, 256), (256, 512)]
+EXC_ON_VECTOR = 3
+FUSED_SLOTS = 2
+HALVES = [(0, 256), (256, 512)]
+PIECES = [(0, 256), (256, 384), (384, 512)]
 
 
-def tile_picked_ynewsv_mov_p_kernel(tc, x_words, x_scales, w1_words, w1_scales, w2_words, w2_scales, pen, unit,
-                        w3_words, w3_scales, offs, nb1, nb2, out):
+def tile_picked_ynewsv_mov_p_kernel(
+        tc, x_words, x_scales, w1_words, w1_scales, w2_words, w2_scales, pen, unit, w3_words, w3_scales,
+        offs, nb1, nb2, out):
     nc = tc.nc
     with ExitStack() as ctx:
         lists = ctx.enter_context(tc.tile_pool(name="lists", bufs=1))
         keep = ctx.enter_context(tc.tile_pool(name="keep", bufs=1))
         psum = ctx.enter_context(tc.psum_pool(name="psum", bufs=1))
 
-        offs_t = lists.tile([P, S // 16], U16, name="offs_t")
-        nb1_t = lists.tile([P, S // 16], U16, name="nb1_t")
-        nb2_t = lists.tile([P, S // 16], U16, name="nb2_t")
-
-        xw = keep.tile([P, PASSES, T], I32, name="xw", align_bytes=64)
-        xs = keep.tile([P, PASSES, T], U8, name="xs", align_bytes=64)
-        ww = [keep.tile([P, PASSES, 2 * H], U8, name=f"ww{m}", align_bytes=64) for m in range(2)]
-        ws = [keep.tile([P, PASSES, H], U8, name=f"ws{m}", align_bytes=64) for m in range(2)]
-        w3w = keep.tile([P, 2 * N], U8, name="w3w", align_bytes=64)
-        w3s = keep.tile([P, N], U8, name="w3s", align_bytes=64)
+        offs_t = lists.tile([P, S // GROUP], U16, name="offs_t")
+        nb1_t = lists.tile([P, S // GROUP], U16, name="nb1_t")
+        nb2_t = lists.tile([P, S // GROUP], U16, name="nb2_t")
+        x_word = keep.tile([P, PASSES, T], I32, name="x_word", align_bytes=64)
+        x_scale = keep.tile([P, PASSES, T], U8, name="x_scale", align_bytes=64)
+        w_word = [keep.tile([P, PASSES, 2 * H], U8, name=f"w_word{m}", align_bytes=64) for m in (DEMAND, STOCK)]
+        w_scale = [keep.tile([P, PASSES, H], U8, name=f"w_scale{m}", align_bytes=64) for m in (DEMAND, STOCK)]
+        w3_word = keep.tile([P, 2 * N], U8, name="w3_word", align_bytes=64)
+        w3_scale = keep.tile([P, 1, N], U8, name="w3_scale", align_bytes=64)
         pen_t = keep.tile([P, PACK], F32, name="pen_t")
         unit_t = keep.tile([P, PACK], F32, name="unit_t")
 
-        def load_scales(queue, plane, src, quads):
-            for q in quads:
-                queue.dma_start(out=plane[32 * q:32 * q + 4].bitcast(I32),
-                                in_=src[:, 4 * q:4 * q + 4, :].rearrange("o r c -> r o c").bitcast(I32))
+        def load_scales(tile, src):
+            for q in range(QUADRANTS):
+                nc.sync.dma_start(out=tile[32 * q:32 * q + 4].bitcast(I32),
+                                  in_=src[:, 4 * q:4 * q + 4, :].rearrange("o r c -> r o c").bitcast(I32))
 
-        def load_words():
-            nc.sync.dma_start(out=xw[:], in_=x_words.rearrange("o p c t -> p o (c t)").bitcast(I32))
+        def load_weight(m, words, scale_bytes):
+            nc.sync.dma_start(out=w_word[m][:].bitcast(I32), in_=words.rearrange("o p c -> p o c").bitcast(I32))
+            load_scales(w_scale[m], scale_bytes)
 
-        def load_w(queue, m, src):
-            queue.dma_start(out=ww[m][:].bitcast(I32), in_=src.rearrange("o p c -> p o c").bitcast(I32))
+        for tile in (x_scale, w_scale[STOCK], w_scale[DEMAND], w3_scale):
+            nc.vector.memset(tile[:].bitcast(I32), 0)
 
-        nc.vector.memset(xs[:].bitcast(I32), 0)
-        nc.vector.memset(ws[1][:].bitcast(I32), 0)
-        nc.vector.memset(ws[0][:].bitcast(I32), 0)
-        nc.vector.memset(w3s[:].bitcast(I32), 0)
         nc.sync.dma_start(offs_t[:], offs)
         nc.sync.dma_start(nb2_t[:], nb2)
-        load_scales(nc.sync, xs, x_scales, range(4))
-        load_words()
-        load_w(nc.sync, 1, w2_words)
-        load_scales(nc.sync, ws[1], w2_scales, range(4))
-        load_w(nc.sync, 0, w1_words)
-        load_scales(nc.sync, ws[0], w1_scales, range(4))
+        load_scales(x_scale, x_scales)
+        nc.sync.dma_start(out=x_word[:], in_=x_words.rearrange("o p c r -> p o (c r)").bitcast(I32))
+        load_weight(STOCK, w2_words, w2_scales)
+        load_weight(DEMAND, w1_words, w1_scales)
         nc.sync.dma_start(nb1_t[:], nb1)
         nc.sync.dma_start(out=pen_t[:], in_=pen.rearrange("(p t) one -> p (t one)", t=PACK))
         nc.sync.dma_start(out=unit_t[:], in_=unit.rearrange("(p t) one -> p (t one)", t=PACK))
-        nc.sync.dma_start(out=w3w[:].bitcast(I32), in_=w3_words[0].bitcast(I32))
-        for q in range(4):
-            nc.sync.dma_start(out=w3s[32 * q:32 * q + 4, :].bitcast(I32), in_=w3_scales[0, 4 * q:4 * q + 4, :].bitcast(I32))
+        nc.sync.dma_start(out=w3_word[:].bitcast(I32), in_=w3_words[0].bitcast(I32))
+        load_scales(w3_scale, w3_scales)
 
         ident = keep.tile([P, P], F32, name="ident")
         nc.vector.memset(ident[:], 0.0)
@@ -87,201 +92,157 @@ def tile_picked_ynewsv_mov_p_kernel(tc, x_words, x_scales, w1_words, w1_scales, 
             nc.vector.memset(exc[t][:, S:], 0.0)
             nc.vector.memset(cost[t][:, S:], 0.0)
 
-        c_gap = keep.tile([P, PACK], F32, name="c_gap")
-        c_met = keep.tile([P, PACK], F32, name="c_met")
-        c_cost = keep.tile([P, PACK], F32, name="c_cost")
-        nc.gpsimd.tensor_scalar(c_gap[:], pen_t[:], 1.25, 0.0, ALU.mult, ALU.add)
-        nc.gpsimd.tensor_scalar(c_met[:], pen_t[:], -1.25, 0.625, ALU.mult, ALU.add)
-        nc.gpsimd.tensor_scalar(c_cost[:], unit_t[:], -0.24, 0.0, ALU.mult, ALU.add)
+        of_gap = keep.tile([P, PACK], F32, name="of_gap")
+        of_low = keep.tile([P, PACK], F32, name="of_low")
+        of_cost = keep.tile([P, PACK], F32, name="of_cost")
+        nc.gpsimd.tensor_scalar(of_gap[:], pen_t[:], 1.25, 0.0, ALU.mult, ALU.add)
+        nc.gpsimd.tensor_scalar(of_low[:], pen_t[:], -1.25, 0.625, ALU.mult, ALU.add)
+        nc.gpsimd.tensor_scalar(of_cost[:], unit_t[:], -0.24, 0.0, ALU.mult, ALU.add)
 
-        gw = [keep.tile([P, S], U32, name=f"gw{o}", align_bytes=64) for o in range(PASSES)]
-        gs = [keep.tile([P, S], U8, name=f"gs{o}", align_bytes=64) for o in range(PASSES)]
+        def entries(list_tile, lo, hi):
+            return list_tile[:, lo // GROUP:hi // GROUP]
+
+        picked_word = [keep.tile([P, S], U32, name=f"picked_word{o}", align_bytes=64) for o in range(PASSES)]
+        picked_scale = [keep.tile([P, S], U8, name=f"picked_scale{o}", align_bytes=64) for o in range(PASSES)]
         for o in range(PASSES):
-            nc.vector.tensor_copy(gs[o][:], xs[:, o, :].indirect(offs_t[:]))
-        for lo, hi in [(0, 128), (128, 256), (256, 512)]:
+            nc.vector.tensor_copy(picked_scale[o][:], x_scale[:, o, :].indirect(offs_t[:]))
+        for lo, hi in WORD_SPANS:
             for o in range(PASSES):
-                nc.vector.tensor_copy(gw[o][:, lo:hi], xw[:, o, :].bitcast(U32).indirect(offs_t[:, lo // 16:hi // 16]))
+                nc.vector.tensor_copy(picked_word[o][:, lo:hi],
+                                      x_word[:, o, :].bitcast(U32).indirect(entries(offs_t, lo, hi)))
 
-        acc = {}
+        prod = {}
         for b in range(BLOCKS):
-            for m in range(2):
-                acc[m, b] = psum.tile([P, H], F32, name=f"acc{m}{b}", tag=f"bank{2 * b + m}")
-        def product(m, b, o):
-            cols = slice(b * P, (b + 1) * P)
-            nc.tensor.matmul_mx(out=acc[m, b][:], lhsT=gw[o][:, cols].bitcast(FP8X4), lhsT_scale=gs[o][:, cols],
-                                rhs=ww[m][:, o, :].bitcast(FP4X4), rhs_scale=ws[m][:, o, :],
-                                start=(o == 0), stop=(o == PASSES - 1))
-
-        for m in (1, 0):
+            for m in (DEMAND, STOCK):
+                prod[m, b] = psum.tile([P, H], F32, name=f"prod{m}{b}", tag=f"bank{2 * b + m}")
+        for m in (STOCK, DEMAND):
             for b in range(BLOCKS):
+                stores = slice(b * P, (b + 1) * P)
                 for o in range(PASSES):
-                    product(m, b, o)
+                    nc.tensor.matmul_mx(out=prod[m, b][:],
+                                        lhsT=picked_word[o][:, stores].bitcast(FP8X4), lhsT_scale=picked_scale[o][:, stores],
+                                        rhs=w_word[m][:, o, :].bitcast(FP4X4), rhs_scale=w_scale[m][:, o, :],
+                                        start=(o == 0), stop=(o == PASSES - 1))
 
-        def dealt(m, b):
-            return acc[m, b][:].rearrange("j (p t) -> j t p", t=PACK)
+        def by_slot(m, b):
+            return prod[m, b][:].rearrange("j (p t) -> j t p", t=PACK)
 
         sig = keep.tile([P, 2, BLOCKS, PACK, P], F32, name="sig")
-        lns = [keep.tile([P, 2, BLOCKS * P], F32, name=f"lns{t}") for t in range(PACK)]
-        soft = [keep.tile([P, 2, BLOCKS * P], F32, name=f"soft{t}") for t in range(PACK)]
-        over_b = [keep.tile([P, PACK, P], F32, name=f"over_b{b}") for b in range(BLOCKS)]
+        sig_stock = [keep.tile([P, PACK, P], F32, name=f"sig_stock{b}") for b in range(BLOCKS)]
+        top_stock = [keep.tile([P, PACK, P], F32, name=f"top_stock{b}") for b in range(BLOCKS)]
         over = [keep.tile([P, PACK, P], F32, name=f"over{b}") for b in range(BLOCKS)]
-        for m in (1, 0):
-            for b in range(BLOCKS):
-                nc.scalar.activation(sig[:, m, b], dealt(m, b), ACT.Sigmoid, scale=-1.0)
         for b in range(BLOCKS):
-            nc.vector.tensor_scalar(over_b[b][:], dealt(1, b), KNEE, None, ALU.max)
+            nc.scalar.activation(sig_stock[b][:], by_slot(STOCK, b), ACT.Sigmoid, scale=-1.0)
         for b in range(BLOCKS):
-            nc.vector.scalar_tensor_tensor(over[b][:], dealt(0, b), KNEE, over_b[b][:], ALU.max, ALU.subtract)
+            nc.scalar.activation(sig[:, DEMAND, b], by_slot(DEMAND, b), ACT.Sigmoid, scale=-1.0)
+        for b in range(BLOCKS):
+            nc.vector.tensor_scalar(top_stock[b][:], by_slot(STOCK, b), KNEE, None, ALU.max)
+            nc.vector.tensor_scalar(sig[:, STOCK, b], sig_stock[b][:], math.exp(-KNEE), None, ALU.max)
+        for b in range(BLOCKS):
+            nc.vector.scalar_tensor_tensor(over[b][:], by_slot(DEMAND, b), KNEE, top_stock[b][:], ALU.max, ALU.subtract)
 
-        gap = [psum.tile([P, S], F32, name=f"gap{t}", tag=f"bank{2 * t + 1}") for t in range(PACK)]
+        gap = [psum.tile([P, S], F32, name=f"gap{t}", tag=f"bank{2 * t + STOCK}") for t in range(PACK)]
+
+        def add_turned(t, b, part, start=False, stop=False):
+            nc.tensor.matmul(gap[t][:, b * P:(b + 1) * P], part, ident[:], start=start, stop=stop, is_transpose=True)
+
         for b in range(BLOCKS):
             for t in range(PACK):
-                nc.tensor.matmul(gap[t][:, b * P:(b + 1) * P], over[b][:, t, :], ident[:], start=(b == 0), stop=False, is_transpose=True)
+                add_turned(t, b, over[b][:, t, :], start=(b == 0))
 
-        def logs(t):
-            nc.scalar.activation(lns[t][:].rearrange("j m (b p) -> j m b p", p=P), sig[:, :, :, t, :], ACT.Ln, bias=FLOOR)
-            nc.vector.tensor_scalar(soft[t][:, 0], lns[t][:, 0], -1.0, KNEE, ALU.mult, ALU.min)
-            nc.vector.tensor_scalar(soft[t][:, 1], lns[t][:, 1], -KNEE, None, ALU.max)
-            for m in range(2):
-                for b in range(BLOCKS):
-                    nc.tensor.matmul(gap[t][:, b * P:(b + 1) * P], soft[t][:, m, b * P:(b + 1) * P], ident[:], start=False,
-                                     stop=(m == 1 and b == BLOCKS - 1), is_transpose=True)
+        logs = [keep.tile([P, 2, BLOCKS, P], F32, name=f"logs{t}") for t in range(PACK)]
+        soft_demand = [keep.tile([P, BLOCKS, P], F32, name=f"soft_demand{t}") for t in range(PACK)]
+        for t in range(PACK):
+            nc.scalar.activation(logs[t][:], sig[:, :, :, t, :], ACT.Ln, bias=FLOOR)
+            nc.vector.tensor_scalar(soft_demand[t][:], logs[t][:, DEMAND], -1.0, KNEE, ALU.mult, ALU.min)
+            for b in range(BLOCKS):
+                add_turned(t, b, logs[t][:, STOCK, b, :])
+            for b in range(BLOCKS):
+                add_turned(t, b, soft_demand[t][:, b, :], stop=(b == BLOCKS - 1))
 
-        first = [keep.tile([P, S], F32, name=f"first{t}") for t in range(PACK)]
-        half2 = [keep.tile([P, S], F32, name=f"half2_{t}") for t in range(PACK)]
-        offer = [keep.tile([P, S], F32, name=f"offer{t}") for t in range(PACK)]
-        base = [keep.tile([P, S], F32, name=f"base{t}") for t in range(PACK)]
-        low = [keep.tile([P, S], F32, name=f"low{t}") for t in range(PACK)]
-        met = [keep.tile([P, S], F32, name=f"met{t}") for t in range(PACK)]
-        far = [keep.tile([P, S], F32, name=f"far{t}") for t in range(PACK)]
-        chunks = [(0, 256), (256, 384), (384, 512)]
-        hid = [keep.tile([P, PACK, hi - lo], BF16, name=f"hid{lo}") for lo, hi in [(0, 256), (256, 512)]]
-        spans = [(0, 256), (256, 512)]
+        def slot_tiles(name, slots):
+            return {t: keep.tile([P, S], F32, name=f"{name}{t}") for t in slots}
 
-        def exc_s(t):
-            nc.scalar.activation(exc[t][:, :S], gap[t][:], ACT.Relu, scale=-1.0)
+        first = slot_tiles("first", range(FUSED_SLOTS, PACK))
+        second = slot_tiles("second", range(PACK))
+        offer = slot_tiles("offer", range(PACK))
+        base = slot_tiles("base", range(PACK))
+        low = slot_tiles("low", range(PACK))
+        met = slot_tiles("met", range(PACK))
+        far = slot_tiles("far", range(PACK))
 
-        def exc_v(t):
-            nc.vector.tensor_scalar(exc[t][:, :S], gap[t][:], -1.0, 0.0, ALU.mult, ALU.max)
+        for t in range(PACK):
+            if t < EXC_ON_VECTOR:
+                nc.vector.tensor_scalar(exc[t][:, :S], gap[t][:], -1.0, 0.0, ALU.mult, ALU.max)
+            else:
+                nc.scalar.activation(exc[t][:, :S], gap[t][:], ACT.Relu, scale=-1.0)
+            nc.scalar.activation(second[t][:], exc[t][:].indirect(nb2_t[:]), ACT.Copy, scale=0.5)
+            if t >= FUSED_SLOTS:
+                nc.scalar.activation(first[t][:], exc[t][:].indirect(nb1_t[:]), ACT.Copy)
 
-        def half_s(t):
-            nc.scalar.activation(half2[t][:], exc[t][:].indirect(nb2_t[:]), ACT.Copy, scale=0.5)
+        def make_base(t):
+            nc.vector.scalar_tensor_tensor(base[t][:], gap[t][:], of_gap[:, t:t + 1], exc[t][:, :S], ALU.mult, ALU.add)
 
-        def first_s(t):
-            nc.scalar.activation(first[t][:], exc[t][:].indirect(nb1_t[:]), ACT.Copy)
+        def make_offer(t):
+            neighbour = exc[t][:].indirect(nb1_t[:]) if t < FUSED_SLOTS else first[t][:]
+            nc.vector.tensor_tensor(offer[t][:], neighbour, second[t][:], ALU.add)
 
-        def second_v(t):
-            nc.vector.tensor_copy(half2[t][:], exc[t][:].indirect(nb2_t[:]))
+        def make_cost(t):
+            nc.vector.scalar_tensor_tensor(cost[t][:, :S], low[t][:], of_low[:, t:t + 1], base[t][:], ALU.mult, ALU.add)
 
-        def offer_join(t):
-            nc.vector.scalar_tensor_tensor(offer[t][:], half2[t][:], 0.5, first[t][:], ALU.mult, ALU.add)
-
-        def offer_add(t):
-            nc.vector.tensor_tensor(offer[t][:], half2[t][:], first[t][:], ALU.add)
-
-        def offer_v(t):
-            nc.vector.tensor_tensor(offer[t][:], exc[t][:].indirect(nb1_t[:]), half2[t][:], ALU.add)
-
-        def based(t):
-            nc.vector.scalar_tensor_tensor(base[t][:], gap[t][:], c_gap[:, t:t + 1], exc[t][:, :S], ALU.mult, ALU.add)
-
-        def meet(t):
+        make_base(0)
+        for t in range(PACK):
+            make_offer(t)
+            if t > 0:
+                make_cost(t - 1)
+            if t + 1 < PACK:
+                make_base(t + 1)
             nc.vector.tensor_tensor(low[t][:], gap[t][:], offer[t][:], ALU.min)
+        make_cost(PACK - 1)
 
-        def price(t):
-            nc.vector.scalar_tensor_tensor(cost[t][:, :S], low[t][:], c_met[:, t:t + 1], base[t][:], ALU.mult, ALU.add)
-
-        def metu(t):
+        for t in range(PACK):
+            for lo, hi in (HALVES if t == PACK - 1 else [(0, S)]):
+                nc.scalar.activation(far[t][:, lo:hi], cost[t][:].indirect(entries(nb1_t, lo, hi)), ACT.Copy)
+        for t in range(PACK):
             nc.vector.tensor_scalar(met[t][:], low[t][:], 0.0, unit_t[:, t:t + 1], ALU.max, ALU.mult)
 
-        def fetch(t, lo=0, hi=S):
-            nc.scalar.activation(far[t][:, lo:hi], cost[t][:].indirect(nb1_t[:, lo // 16:hi // 16]), ACT.Copy)
+        hid = [keep.tile([P, PACK, hi - lo], BF16, name=f"hid{lo}") for lo, hi in HALVES]
+        woven = [keep.tile([P, hi - lo, PACK], BF16, name=f"woven{lo}", align_bytes=64) for lo, hi in PIECES]
+        hid_word = [keep.tile([P, hi - lo], U32, name=f"hid_word{lo}", align_bytes=64) for lo, hi in PIECES]
+        hid_scale = [keep.tile([P, hi - lo], U8, name=f"hid_scale{lo}", align_bytes=64) for lo, hi in PIECES]
+        result = [keep.tile([P, N // P, hi - lo], F32, name=f"result{lo}") for lo, hi in PIECES]
 
-        def finish(t, lo=0, hi=S):
-            nc.vector.scalar_tensor_tensor(hid[spans.index((lo, hi))][:, t, :], far[t][:, lo:hi], c_cost[:, t:t + 1], met[t][:, lo:hi], ALU.mult, ALU.add)
+        def finish(half):
+            lo, hi = HALVES[half]
+            for t in range(PACK):
+                nc.vector.scalar_tensor_tensor(hid[half][:, t, :], far[t][:, lo:hi], of_cost[:, t:t + 1], met[t][:, lo:hi],
+                                               ALU.mult, ALU.add)
 
-        woven = [keep.tile([P, hi - lo, PACK], BF16, name=f"woven{lo}", align_bytes=64) for lo, hi in chunks]
-        codes = [keep.tile([P, hi - lo], U32, name=f"codes{lo}", align_bytes=64) for lo, hi in chunks]
-        scales = [keep.tile([P, hi - lo], U8, name=f"scales{lo}", align_bytes=64) for lo, hi in chunks]
-        res = [keep.tile([P, 2, hi - lo], F32, name=f"res{lo}") for lo, hi in chunks]
+        def weave(piece, half, copy):
+            lo, hi = PIECES[piece]
+            at = HALVES[half][0]
+            copy(woven[piece][:].rearrange("p (c i) t -> p c t i", i=RUN),
+                 hid[half][:, :, lo - at:hi - at].rearrange("p t (c i) -> p c t i", i=RUN))
 
-        def part(lo, hi):
-            for i, (a, b) in enumerate(spans):
-                if a <= lo and hi <= b:
-                    return hid[i][:, :, lo - a:hi - a]
+        def multiply(piece, copy):
+            lo, hi = PIECES[piece]
+            nc.vector.quantize_mx(out=hid_word[piece][:].bitcast(FP8X4), scales=hid_scale[piece][:],
+                                  in_=woven[piece][:].rearrange("p j t -> p (j t)"))
+            regions = psum.tile([P, N // P, hi - lo], F32, name=f"regions{lo}", tag=f"bank{2 * piece + DEMAND}")
+            for r in range(N // P):
+                nc.tensor.matmul_mx(out=regions[:, r, :],
+                                    lhsT=w3_word[:, 2 * r * P:2 * (r + 1) * P].bitcast(FP4X4),
+                                    lhsT_scale=w3_scale[:, 0, r * P:(r + 1) * P],
+                                    rhs=hid_word[piece][:].bitcast(FP8X4), rhs_scale=hid_scale[piece][:],
+                                    start=True, stop=True)
+            copy(result[piece][:], regions[:])
+            nc.sync.dma_start(out=out[:, lo:hi].rearrange("(r p) j -> p r j", p=P), in_=result[piece][:])
 
-        def weave(h):
-            lo, hi = chunks[h]
-            nc.vector.tensor_copy(woven[h][:].rearrange("p (c i) t -> p c t i", i=4), part(lo, hi).rearrange("p t (c i) -> p c t i", i=4))
-
-        def weave_s(h):
-            lo, hi = chunks[h]
-            nc.scalar.copy(woven[h][:].rearrange("p (c i) t -> p c t i", i=4), part(lo, hi).rearrange("p t (c i) -> p c t i", i=4))
-
-        def quant_v(h):
-            quant(h, nc.vector.tensor_copy)
-
-        def quant(h, move=nc.scalar.copy):
-            lo, hi = chunks[h]
-            nc.vector.quantize_mx(out=codes[h][:].bitcast(FP8X4), scales=scales[h][:], in_=woven[h][:].rearrange("p j t -> p (j t)"))
-            region = psum.tile([P, 2, hi - lo], F32, name=f"region{h}", tag=f"bank{2 * h}")
-            for r in range(2):
-                nc.tensor.matmul_mx(out=region[:, r, :], lhsT=w3w[:, r * 2 * P:(r + 1) * 2 * P].bitcast(FP4X4),
-                                    lhsT_scale=w3s[:, r * P:(r + 1) * P], rhs=codes[h][:].bitcast(FP8X4),
-                                    rhs_scale=scales[h][:], start=True, stop=True)
-            move(res[h][:], region[:])
-            nc.sync.dma_start(out=out[:, lo:hi].rearrange("(r p) j -> p r j", p=P), in_=res[h][:])
-
-        logs(0)
-        logs(1)
-        logs(2)
-        logs(3)
-        exc_v(0)
-        half_s(0)
-        exc_v(1)
-        based(0)
-        offer_v(0)
-        half_s(1)
-        based(1)
-        meet(0)
-        exc_s(2)
-        half_s(2)
-        first_s(2)
-        offer_v(1)
-        price(0)
-        meet(1)
-        based(2)
-        exc_s(3)
-        half_s(3)
-        first_s(3)
-        price(1)
-        offer_add(2)
-        based(3)
-        meet(2)
-        offer_add(3)
-        price(2)
-        meet(3)
-        price(3)
-        fetch(0)
-        fetch(1)
-        fetch(2)
-        fetch(3,0,256)
-        fetch(3,256,512)
-        metu(0)
-        metu(1)
-        metu(2)
-        metu(3)
-        finish(0,0,256)
-        finish(1,0,256)
-        finish(2,0,256)
-        finish(3,0,256)
-        weave_s(0)
-        finish(0,256,512)
-        finish(1,256,512)
-        finish(2,256,512)
-        finish(3,256,512)
-        weave(1)
-        quant(0)
-        weave(2)
-        quant(1)
-        quant_v(2)
+        finish(0)
+        weave(0, 0, nc.scalar.copy)
+        finish(1)
+        weave(1, 1, nc.vector.tensor_copy)
+        multiply(0, nc.scalar.copy)
+        weave(2, 1, nc.vector.tensor_copy)
+        multiply(1, nc.scalar.copy)
+        multiply(2, nc.vector.tensor_copy)

import math
from contextlib import ExitStack

import concourse.mybir as mybir
from concourse.masks import make_identity

F32 = mybir.dt.float32
BF16 = mybir.dt.bfloat16
I32 = mybir.dt.int32
U32 = mybir.dt.uint32
U16 = mybir.dt.uint16
U8 = mybir.dt.uint8
FP8X4 = mybir.dt.float8_e4m3fn_x4
FP4X4 = mybir.dt.float4_e2m1fn_x4
ALU = mybir.AluOpType
ACT = mybir.ActivationFunctionType

K, T, S, N, H = 1024, 1024, 512, 256, 512
FLOPS = 2 * (2 * K * H * S + H * N * S)

P = 128
PACK = 4
PASSES = K // (P * PACK)
BLOCKS = S // P
QUADRANTS = 4
GROUP = 16
SPARE = 16
DEMAND, STOCK = 0, 1
KNEE = 20.0
FLOOR = 2.0 ** -60
RUN = 4

WORD_SPANS = [(0, 128), (128, 256), (256, 512)]
EXC_ON_VECTOR = 3
FUSED_SLOTS = 2
HALVES = [(0, 256), (256, 512)]
PIECES = [(0, 256), (256, 384), (384, 512)]


def tile_picked_ynewsv_mov_p_kernel(
        tc, x_words, x_scales, w1_words, w1_scales, w2_words, w2_scales, pen, unit, w3_words, w3_scales,
        offs, nb1, nb2, out):
    nc = tc.nc
    with ExitStack() as ctx:
        lists = ctx.enter_context(tc.tile_pool(name="lists", bufs=1))
        keep = ctx.enter_context(tc.tile_pool(name="keep", bufs=1))
        psum = ctx.enter_context(tc.psum_pool(name="psum", bufs=1))

        offs_t = lists.tile([P, S // GROUP], U16, name="offs_t")
        nb1_t = lists.tile([P, S // GROUP], U16, name="nb1_t")
        nb2_t = lists.tile([P, S // GROUP], U16, name="nb2_t")
        x_word = keep.tile([P, PASSES, T], I32, name="x_word", align_bytes=64)
        x_scale = keep.tile([P, PASSES, T], U8, name="x_scale", align_bytes=64)
        w_word = [keep.tile([P, PASSES, 2 * H], U8, name=f"w_word{m}", align_bytes=64) for m in (DEMAND, STOCK)]
        w_scale = [keep.tile([P, PASSES, H], U8, name=f"w_scale{m}", align_bytes=64) for m in (DEMAND, STOCK)]
        w3_word = keep.tile([P, 2 * N], U8, name="w3_word", align_bytes=64)
        w3_scale = keep.tile([P, 1, N], U8, name="w3_scale", align_bytes=64)
        pen_t = keep.tile([P, PACK], F32, name="pen_t")
        unit_t = keep.tile([P, PACK], F32, name="unit_t")

        def load_scales(tile, src):
            for q in range(QUADRANTS):
                nc.sync.dma_start(out=tile[32 * q:32 * q + 4].bitcast(I32),
                                  in_=src[:, 4 * q:4 * q + 4, :].rearrange("o r c -> r o c").bitcast(I32))

        def load_weight(m, words, scale_bytes):
            nc.sync.dma_start(out=w_word[m][:].bitcast(I32), in_=words.rearrange("o p c -> p o c").bitcast(I32))
            load_scales(w_scale[m], scale_bytes)

        for tile in (x_scale, w_scale[STOCK], w_scale[DEMAND], w3_scale):
            nc.vector.memset(tile[:].bitcast(I32), 0)

        nc.sync.dma_start(offs_t[:], offs)
        nc.sync.dma_start(nb2_t[:], nb2)
        load_scales(x_scale, x_scales)
        nc.sync.dma_start(out=x_word[:], in_=x_words.rearrange("o p c r -> p o (c r)").bitcast(I32))
        load_weight(STOCK, w2_words, w2_scales)
        load_weight(DEMAND, w1_words, w1_scales)
        nc.sync.dma_start(nb1_t[:], nb1)
        nc.sync.dma_start(out=pen_t[:], in_=pen.rearrange("(p t) one -> p (t one)", t=PACK))
        nc.sync.dma_start(out=unit_t[:], in_=unit.rearrange("(p t) one -> p (t one)", t=PACK))
        nc.sync.dma_start(out=w3_word[:].bitcast(I32), in_=w3_words[0].bitcast(I32))
        load_scales(w3_scale, w3_scales)

        ident = keep.tile([P, P], F32, name="ident")
        nc.vector.memset(ident[:], 0.0)
        make_identity(nc, ident[:], nomemset=True)

        exc = [keep.tile([P, S + SPARE], F32, name=f"exc{t}") for t in range(PACK)]
        cost = [keep.tile([P, S + SPARE], F32, name=f"cost{t}") for t in range(PACK)]
        for t in range(PACK):
            nc.vector.memset(exc[t][:, S:], 0.0)
            nc.vector.memset(cost[t][:, S:], 0.0)

        of_gap = keep.tile([P, PACK], F32, name="of_gap")
        of_low = keep.tile([P, PACK], F32, name="of_low")
        of_cost = keep.tile([P, PACK], F32, name="of_cost")
        nc.gpsimd.tensor_scalar(of_gap[:], pen_t[:], 1.25, 0.0, ALU.mult, ALU.add)
        nc.gpsimd.tensor_scalar(of_low[:], pen_t[:], -1.25, 0.625, ALU.mult, ALU.add)
        nc.gpsimd.tensor_scalar(of_cost[:], unit_t[:], -0.24, 0.0, ALU.mult, ALU.add)

        def entries(list_tile, lo, hi):
            return list_tile[:, lo // GROUP:hi // GROUP]

        picked_word = [keep.tile([P, S], U32, name=f"picked_word{o}", align_bytes=64) for o in range(PASSES)]
        picked_scale = [keep.tile([P, S], U8, name=f"picked_scale{o}", align_bytes=64) for o in range(PASSES)]
        for o in range(PASSES):
            nc.vector.tensor_copy(picked_scale[o][:], x_scale[:, o, :].indirect(offs_t[:]))
        for lo, hi in WORD_SPANS:
            for o in range(PASSES):
                nc.vector.tensor_copy(picked_word[o][:, lo:hi],
                                      x_word[:, o, :].bitcast(U32).indirect(entries(offs_t, lo, hi)))

        prod = {}
        for b in range(BLOCKS):
            for m in (DEMAND, STOCK):
                prod[m, b] = psum.tile([P, H], F32, name=f"prod{m}{b}", tag=f"bank{2 * b + m}")
        for m in (STOCK, DEMAND):
            for b in range(BLOCKS):
                stores = slice(b * P, (b + 1) * P)
                for o in range(PASSES):
                    nc.tensor.matmul_mx(out=prod[m, b][:],
                                        lhsT=picked_word[o][:, stores].bitcast(FP8X4), lhsT_scale=picked_scale[o][:, stores],
                                        rhs=w_word[m][:, o, :].bitcast(FP4X4), rhs_scale=w_scale[m][:, o, :],
                                        start=(o == 0), stop=(o == PASSES - 1))

        def by_slot(m, b):
            return prod[m, b][:].rearrange("j (p t) -> j t p", t=PACK)

        sig = keep.tile([P, 2, BLOCKS, PACK, P], F32, name="sig")
        sig_stock = [keep.tile([P, PACK, P], F32, name=f"sig_stock{b}") for b in range(BLOCKS)]
        top_stock = [keep.tile([P, PACK, P], F32, name=f"top_stock{b}") for b in range(BLOCKS)]
        over = [keep.tile([P, PACK, P], F32, name=f"over{b}") for b in range(BLOCKS)]
        for b in range(BLOCKS):
            nc.scalar.activation(sig_stock[b][:], by_slot(STOCK, b), ACT.Sigmoid, scale=-1.0)
        for b in range(BLOCKS):
            nc.scalar.activation(sig[:, DEMAND, b], by_slot(DEMAND, b), ACT.Sigmoid, scale=-1.0)
        for b in range(BLOCKS):
            nc.vector.tensor_scalar(top_stock[b][:], by_slot(STOCK, b), KNEE, None, ALU.max)
            nc.vector.tensor_scalar(sig[:, STOCK, b], sig_stock[b][:], math.exp(-KNEE), None, ALU.max)
        for b in range(BLOCKS):
            nc.vector.scalar_tensor_tensor(over[b][:], by_slot(DEMAND, b), KNEE, top_stock[b][:], ALU.max, ALU.subtract)

        gap = [psum.tile([P, S], F32, name=f"gap{t}", tag=f"bank{2 * t + STOCK}") for t in range(PACK)]

        def add_turned(t, b, part, start=False, stop=False):
            nc.tensor.matmul(gap[t][:, b * P:(b + 1) * P], part, ident[:], start=start, stop=stop, is_transpose=True)

        for b in range(BLOCKS):
            for t in range(PACK):
                add_turned(t, b, over[b][:, t, :], start=(b == 0))

        logs = [keep.tile([P, 2, BLOCKS, P], F32, name=f"logs{t}") for t in range(PACK)]
        soft_demand = [keep.tile([P, BLOCKS, P], F32, name=f"soft_demand{t}") for t in range(PACK)]
        for t in range(PACK):
            nc.scalar.activation(logs[t][:], sig[:, :, :, t, :], ACT.Ln, bias=FLOOR)
            nc.vector.tensor_scalar(soft_demand[t][:], logs[t][:, DEMAND], -1.0, KNEE, ALU.mult, ALU.min)
            for b in range(BLOCKS):
                add_turned(t, b, logs[t][:, STOCK, b, :])
            for b in range(BLOCKS):
                add_turned(t, b, soft_demand[t][:, b, :], stop=(b == BLOCKS - 1))

        def slot_tiles(name, slots):
            return {t: keep.tile([P, S], F32, name=f"{name}{t}") for t in slots}

        first = slot_tiles("first", range(FUSED_SLOTS, PACK))
        second = slot_tiles("second", range(PACK))
        offer = slot_tiles("offer", range(PACK))
        base = slot_tiles("base", range(PACK))
        low = slot_tiles("low", range(PACK))
        met = slot_tiles("met", range(PACK))
        far = slot_tiles("far", range(PACK))

        for t in range(PACK):
            if t < EXC_ON_VECTOR:
                nc.vector.tensor_scalar(exc[t][:, :S], gap[t][:], -1.0, 0.0, ALU.mult, ALU.max)
            else:
                nc.scalar.activation(exc[t][:, :S], gap[t][:], ACT.Relu, scale=-1.0)
            nc.scalar.activation(second[t][:], exc[t][:].indirect(nb2_t[:]), ACT.Copy, scale=0.5)
            if t >= FUSED_SLOTS:
                nc.scalar.activation(first[t][:], exc[t][:].indirect(nb1_t[:]), ACT.Copy)

        def make_base(t):
            nc.vector.scalar_tensor_tensor(base[t][:], gap[t][:], of_gap[:, t:t + 1], exc[t][:, :S], ALU.mult, ALU.add)

        def make_offer(t):
            neighbour = exc[t][:].indirect(nb1_t[:]) if t < FUSED_SLOTS else first[t][:]
            nc.vector.tensor_tensor(offer[t][:], neighbour, second[t][:], ALU.add)

        def make_cost(t):
            nc.vector.scalar_tensor_tensor(cost[t][:, :S], low[t][:], of_low[:, t:t + 1], base[t][:], ALU.mult, ALU.add)

        make_base(0)
        for t in range(PACK):
            make_offer(t)
            if t > 0:
                make_cost(t - 1)
            if t + 1 < PACK:
                make_base(t + 1)
            nc.vector.tensor_tensor(low[t][:], gap[t][:], offer[t][:], ALU.min)
        make_cost(PACK - 1)

        for t in range(PACK):
            for lo, hi in (HALVES if t == PACK - 1 else [(0, S)]):
                nc.scalar.activation(far[t][:, lo:hi], cost[t][:].indirect(entries(nb1_t, lo, hi)), ACT.Copy)
        for t in range(PACK):
            nc.vector.tensor_scalar(met[t][:], low[t][:], 0.0, unit_t[:, t:t + 1], ALU.max, ALU.mult)

        hid = [keep.tile([P, PACK, hi - lo], BF16, name=f"hid{lo}") for lo, hi in HALVES]
        woven = [keep.tile([P, hi - lo, PACK], BF16, name=f"woven{lo}", align_bytes=64) for lo, hi in PIECES]
        hid_word = [keep.tile([P, hi - lo], U32, name=f"hid_word{lo}", align_bytes=64) for lo, hi in PIECES]
        hid_scale = [keep.tile([P, hi - lo], U8, name=f"hid_scale{lo}", align_bytes=64) for lo, hi in PIECES]
        result = [keep.tile([P, N // P, hi - lo], F32, name=f"result{lo}") for lo, hi in PIECES]

        def finish(half):
            lo, hi = HALVES[half]
            for t in range(PACK):
                nc.vector.scalar_tensor_tensor(hid[half][:, t, :], far[t][:, lo:hi], of_cost[:, t:t + 1], met[t][:, lo:hi],
                                               ALU.mult, ALU.add)

        def weave(piece, half, copy):
            lo, hi = PIECES[piece]
            at = HALVES[half][0]
            copy(woven[piece][:].rearrange("p (c i) t -> p c t i", i=RUN),
                 hid[half][:, :, lo - at:hi - at].rearrange("p t (c i) -> p c t i", i=RUN))

        def multiply(piece, copy):
            lo, hi = PIECES[piece]
            nc.vector.quantize_mx(out=hid_word[piece][:].bitcast(FP8X4), scales=hid_scale[piece][:],
                                  in_=woven[piece][:].rearrange("p j t -> p (j t)"))
            regions = psum.tile([P, N // P, hi - lo], F32, name=f"regions{lo}", tag=f"bank{2 * piece + DEMAND}")
            for r in range(N // P):
                nc.tensor.matmul_mx(out=regions[:, r, :],
                                    lhsT=w3_word[:, 2 * r * P:2 * (r + 1) * P].bitcast(FP4X4),
                                    lhsT_scale=w3_scale[:, 0, r * P:(r + 1) * P],
                                    rhs=hid_word[piece][:].bitcast(FP8X4), rhs_scale=hid_scale[piece][:],
                                    start=True, stop=True)
            copy(result[piece][:], regions[:])
            nc.sync.dma_start(out=out[:, lo:hi].rearrange("(r p) j -> p r j", p=P), in_=result[piece][:])

        finish(0)
        weave(0, 0, nc.scalar.copy)
        finish(1)
        weave(1, 1, nc.vector.tensor_copy)
        multiply(0, nc.scalar.copy)
        weave(2, 1, nc.vector.tensor_copy)
        multiply(1, nc.scalar.copy)
        multiply(2, nc.vector.tensor_copy)
